import numpy as np, ml_dtypes
CORES = [30,158,46,174,86,214]
N = 6
KB, QP = 1, 32
MEM = [0,5]
def setup_inputs(rng):
    return {"q": rng.standard_normal((N, 128, QP), dtype=np.float32).astype(ml_dtypes.bfloat16), "k": rng.standard_normal((N, 128, KB * 128), dtype=np.float32).astype(ml_dtypes.bfloat16), "v": rng.standard_normal((N, 128, KB * 128), dtype=np.float32).astype(ml_dtypes.bfloat16)}
def setup_inputs_big(rng):
    d = setup_inputs(rng)
    for k in ("q", "k", "v"): d[k] = (d[k].astype(np.float32) * 1024.0).astype(d[k].dtype)
    return d
def setup_inputs_small(rng):
    d = setup_inputs(rng)
    for k in ("q", "k", "v"): d[k] = (d[k].astype(np.float32) * (1 / 1024.0)).astype(d[k].dtype)
    return d
def setup_inputs_apart(rng):
    d = setup_inputs(rng)
    f = (10.0 ** rng.permutation(np.linspace(-1.5, 1.5, N))).astype(np.float32).reshape(N, 1, 1)
    for k in ("q", "k", "v"): d[k] = (d[k].astype(np.float32) * f).astype(d[k].dtype)
    return d
def reference(q, k, v):
    Q, K, V = q.astype(np.float64), k.astype(np.float64), v.astype(np.float64)
    y = np.zeros((N, 128, QP))
    for r in range(N):
        for j in MEM:
            for b in range(KB):
                S = np.maximum(K[j][:, 128 * b:128 * b + 128].T @ Q[r], 0.0)
                y[r] += V[j][:, 128 * b:128 * b + 128].T @ S
    return {"y": y.astype(ml_dtypes.bfloat16 if q.dtype != np.float64 else np.float64)}

@@ -1,0 +1,143 @@
+from concourse.bass import DstId, RemoteDMATransfer
+from concourse.mybir import AluOpType
+
+QP = 32
+KP = 128
+CAP = 2
+W = QP * (1 + CAP)
+
+SCRATCH = {
+    "kv": ("sbuf", [128, 2 * KP], "bfloat16"),
+    "kvo": ("sbuf", [128, 2 * KP], "bfloat16"),
+    "qall": ("sbuf", [128, W], "bfloat16"),
+    "qd": ("dram", [128, QP], "bfloat16"),
+    "zero": ("sbuf", [128, W], "float32"),
+    "sb": ("sbuf", [128, 2 * W], "bfloat16"),
+    "yb": ("sbuf", [128, W], "bfloat16"),
+    "yland": ("dram", [128, QP], "bfloat16"),
+    "ps_a": ("psum", [128, 512], "float32"),
+    "ps_b": ("psum", [128, 512], "float32"),
+    "ps_o": ("psum", [128, 512], "float32"),
+}
+SEMAPHORES = ["ld", "ldq", "zs", "arr_kv", "arr_q", "arr_y", "mm_a", "mm_b", "rl_a", "rl_b", "mm_o", "cp", "sent", "st"]
+
+
+def _engines(mask):
+    return [e for e in range(mask.bit_length()) if (mask >> e) & 1]
+
+
+def _split(mask, parts):
+    eng = _engines(mask)
+    per = 1
+    while per * 2 * parts <= len(eng):
+        per *= 2
+    return [sum(1 << e for e in eng[i * per:(i + 1) * per]) for i in range(parts)]
+
+
+def _plan(T, topo):
+    cores, mem = T.cores, list(T.tables["MEM"])
+    served = {m: [] for m in mem}
+    left = []
+    for r in range(len(cores)):
+        if r in mem:
+            continue
+        near = [m for m in mem if topo.same_plane(cores[r], cores[m]) and len(served[m]) < CAP]
+        if near:
+            served[near[0]].append(r)
+        else:
+            left.append(r)
+    for r in left:
+        served[min(mem, key=lambda m: len(served[m]))].append(r)
+    return mem, served
+
+
+def _y_masks(T, topo, server, clients):
+    common = topo.mask(T.cores[server], T.cores[clients[0]])
+    for c in clients:
+        common &= topo.mask(T.cores[server], T.cores[c])
+    return _split(common, len(clients))
+
+
+def _memory_rank(g, core, T, topo, rank, mem, served):
+    s, cores = T.sem, T.cores
+    other = [m for m in mem if m != rank][0]
+    clients = served[rank]
+    k_own, v_own = T.kv[:, 0:KP], T.kv[:, KP:2 * KP]
+    k_oth, v_oth = T.kvo[:, 0:KP], T.kvo[:, KP:2 * KP]
+
+    g.sync.dma_start(k_own, T.k[:]).then_inc(s.ld, 16)
+    g.scalar.dma_start(v_own, T.v[:]).then_inc(s.ld, 16)
+    g.sync.dma_start(T.qall[:, 0:QP], T.q[:]).then_inc(s.ldq, 16)
+    g.vector.memset(T.zero[:], 0.0).then_inc(s.zs, 1)
+
+    rid, pid = topo.addr(cores[other], core)
+    mk = topo.mask(core, cores[other])
+    g.wait_ge(s.ld, 32)
+    g.remote_dma(out_ap=T.kvo[:], in_ap=T.kv[:], remote_sem=s.arr_kv, local_sem=s.sent,
+                 pid=pid, routing_id=rid, dma_engine_mask=mk)
+    sent = len(_engines(mk))
+
+    n_q = sum(len(_engines(topo.mask(cores[c], core))) for c in clients)
+    n_kv = len(_engines(topo.mask(cores[other], core)))
+    g.tensor.wait_ge(s.ld, 32)
+    g.tensor.wait_ge(s.ldq, 16)
+    g.tensor.wait_ge(s.arr_q, n_q)
+    g.tensor.matmul(T.ps_a[:, 0:W], k_own, T.qall[:], True, True).then_inc(s.mm_a, 1)
+    g.tensor.wait_ge(s.arr_kv, n_kv)
+    g.tensor.matmul(T.ps_b[:, 0:W], k_oth, T.qall[:], True, True).then_inc(s.mm_b, 1)
+    g.tensor.wait_ge(s.rl_a, 1)
+    g.tensor.matmul(T.ps_o[:, 0:W], v_own, T.sb[:, 0:W], True, False)
+    g.tensor.wait_ge(s.rl_b, 1)
+    g.tensor.matmul(T.ps_o[:, 0:W], v_oth, T.sb[:, W:2 * W], False, True).then_inc(s.mm_o, 1)
+
+    g.vector.wait_ge(s.zs, 1)
+    g.vector.wait_ge(s.mm_a, 1)
+    g.vector.tensor_tensor(T.sb[:, 0:W], T.ps_a[:, 0:W], T.zero[:], AluOpType.max).then_inc(s.rl_a, 1)
+    g.vector.wait_ge(s.mm_b, 1)
+    g.vector.tensor_tensor(T.sb[:, W:2 * W], T.ps_b[:, 0:W], T.zero[:], AluOpType.max).then_inc(s.rl_b, 1)
+    g.vector.wait_ge(s.mm_o, 1)
+    g.vector.tensor_copy(T.yb[:], T.ps_o[:, 0:W]).then_inc(s.cp, 1)
+
+    masks = _y_masks(T, topo, rank, clients)
+    transfers = []
+    for i, c in enumerate(clients):
+        rid, pid = topo.addr(cores[c], core)
+        transfers.append(RemoteDMATransfer(dst_ids=[DstId(rid=rid, pnc=pid)], dma_engine_mask=masks[i],
+                                           remote_sem=s.arr_y, src=T.yb[:, (i + 1) * QP:(i + 2) * QP],
+                                           dst=T.yland[:]))
+        sent += len(_engines(masks[i]))
+    g.wait_ge(s.cp, 1)
+    g.remote_dma_fused(transfers, local_sem=s.sent)
+    g.sync.wait_ge(s.cp, 1)
+    g.sync.dma_start(T.y[:], T.yb[:, 0:QP]).then_inc(s.st, 16)
+
+    g.wait_ge(s.sent, sent)
+    g.wait_ge(s.st, 16)
+
+
+def _client(g, core, T, topo, rank, server, clients):
+    s, cores = T.sem, T.cores
+    slot = clients.index(rank)
+    g.sync.dma_start(T.qd[:], T.q[:]).then_inc(s.ldq, 16)
+    rid, pid = topo.addr(cores[server], core)
+    mk = topo.mask(core, cores[server])
+    g.wait_ge(s.ldq, 16)
+    g.remote_dma(out_ap=T.qall[:, (slot + 1) * QP:(slot + 2) * QP], in_ap=T.qd[:], remote_sem=s.arr_q,
+                 local_sem=s.sent, pid=pid, routing_id=rid, dma_engine_mask=mk)
+    n_y = len(_engines(_y_masks(T, topo, server, clients)[slot]))
+    g.sync.wait_ge(s.arr_y, n_y)
+    g.sync.dma_start(T.y[:], T.yland[:]).then_inc(s.st, 16)
+    g.wait_ge(s.sent, len(_engines(mk)))
+    g.wait_ge(s.st, 16)
+
+
+def rank_program(g, core, T, topo):
+    rank = T.rank_of(core)
+    if rank is None:
+        return
+    mem, served = _plan(T, topo)
+    if rank in mem:
+        _memory_rank(g, core, T, topo, rank, mem, served)
+    else:
+        server = [m for m in mem if rank in served[m]][0]
+        _client(g, core, T, topo, rank, server, served[server])

@@ -4,22 +4,30 @@ from concourse.mybir import AluOpType
 QP = 32
 KP = 128
 CAP = 2
-W = QP * (1 + CAP)
+WC = QP * CAP
 
 SCRATCH = {
+    "kd": ("dram", [128, KP], "bfloat16"),
+    "vd": ("dram", [128, KP], "bfloat16"),
     "kv": ("sbuf", [128, 2 * KP], "bfloat16"),
     "kvo": ("sbuf", [128, 2 * KP], "bfloat16"),
-    "qall": ("sbuf", [128, W], "bfloat16"),
+    "qc": ("sbuf", [128, WC], "bfloat16"),
+    "qo": ("sbuf", [128, QP], "bfloat16"),
     "qd": ("dram", [128, QP], "bfloat16"),
-    "zero": ("sbuf", [128, W], "float32"),
-    "sb": ("sbuf", [128, 2 * W], "bfloat16"),
-    "yb": ("sbuf", [128, W], "bfloat16"),
+    "zero": ("sbuf", [128, WC], "float32"),
+    "sb": ("sbuf", [128, 2 * WC], "bfloat16"),
+    "sbo": ("sbuf", [128, 2 * QP], "bfloat16"),
+    "yb": ("sbuf", [128, WC], "bfloat16"),
+    "ybo": ("sbuf", [128, QP], "bfloat16"),
     "yland": ("dram", [128, QP], "bfloat16"),
     "ps_a": ("psum", [128, 512], "float32"),
     "ps_b": ("psum", [128, 512], "float32"),
     "ps_o": ("psum", [128, 512], "float32"),
+    "ps_c": ("psum", [128, 512], "float32"),
+    "ps_p": ("psum", [128, 512], "float32"),
 }
-SEMAPHORES = ["ld", "ldq", "zs", "arr_kv", "arr_q", "arr_y", "mm_a", "mm_b", "rl_a", "rl_b", "mm_o", "cp", "sent", "st"]
+SEMAPHORES = ["stk", "stv", "ldk", "ldv", "ldq", "zs", "arr_k", "arr_v", "arr_q", "arr_y",
+              "mm_a", "mm_b", "rl_a", "rl_b", "mm_o", "cp", "mm_c", "rl_c", "mm_p", "cpo", "sent", "st"]
 
 
 def _engines(mask):
@@ -64,52 +72,70 @@ def _memory_rank(g, core, T, topo, rank, mem, served):
     clients = served[rank]
     k_own, v_own = T.kv[:, 0:KP], T.kv[:, KP:2 * KP]
     k_oth, v_oth = T.kvo[:, 0:KP], T.kvo[:, KP:2 * KP]
+    relu = AluOpType.max
 
-    g.sync.dma_start(k_own, T.k[:]).then_inc(s.ld, 16)
-    g.scalar.dma_start(v_own, T.v[:]).then_inc(s.ld, 16)
-    g.sync.dma_start(T.qall[:, 0:QP], T.q[:]).then_inc(s.ldq, 16)
+    g.sync.dma_start(T.kd[:], T.k[:]).then_inc(s.stk, 16)
+    g.scalar.dma_start(T.vd[:], T.v[:]).then_inc(s.stv, 16)
+    g.sync.dma_start(k_own, T.k[:]).then_inc(s.ldk, 16)
+    g.scalar.dma_start(v_own, T.v[:]).then_inc(s.ldv, 16)
+    g.sync.dma_start(T.qo[:], T.q[:]).then_inc(s.ldq, 16)
     g.vector.memset(T.zero[:], 0.0).then_inc(s.zs, 1)
 
     rid, pid = topo.addr(cores[other], core)
     mk = topo.mask(core, cores[other])
-    g.wait_ge(s.ld, 32)
-    g.remote_dma(out_ap=T.kvo[:], in_ap=T.kv[:], remote_sem=s.arr_kv, local_sem=s.sent,
+    g.wait_ge(s.stk, 16)
+    g.remote_dma(out_ap=k_oth, in_ap=T.kd[:], remote_sem=s.arr_k, local_sem=s.sent,
                  pid=pid, routing_id=rid, dma_engine_mask=mk)
-    sent = len(_engines(mk))
+    g.wait_ge(s.stv, 16)
+    g.remote_dma(out_ap=v_oth, in_ap=T.vd[:], remote_sem=s.arr_v, local_sem=s.sent,
+                 pid=pid, routing_id=rid, dma_engine_mask=mk)
+    sent = 2 * len(_engines(mk))
 
     n_q = sum(len(_engines(topo.mask(cores[c], core))) for c in clients)
     n_kv = len(_engines(topo.mask(cores[other], core)))
-    g.tensor.wait_ge(s.ld, 32)
-    g.tensor.wait_ge(s.ldq, 16)
+
+    g.tensor.wait_ge(s.ldk, 16)
     g.tensor.wait_ge(s.arr_q, n_q)
-    g.tensor.matmul(T.ps_a[:, 0:W], k_own, T.qall[:], True, True).then_inc(s.mm_a, 1)
-    g.tensor.wait_ge(s.arr_kv, n_kv)
-    g.tensor.matmul(T.ps_b[:, 0:W], k_oth, T.qall[:], True, True).then_inc(s.mm_b, 1)
+    g.tensor.matmul(T.ps_a[:, 0:WC], k_own, T.qc[:], True, True).then_inc(s.mm_a, 1)
+    g.tensor.wait_ge(s.arr_k, n_kv)
+    g.tensor.matmul(T.ps_b[:, 0:WC], k_oth, T.qc[:], True, True).then_inc(s.mm_b, 1)
+    g.tensor.wait_ge(s.ldv, 16)
     g.tensor.wait_ge(s.rl_a, 1)
-    g.tensor.matmul(T.ps_o[:, 0:W], v_own, T.sb[:, 0:W], True, False)
+    g.tensor.matmul(T.ps_o[:, 0:WC], v_own, T.sb[:, 0:WC], True, False)
     g.tensor.wait_ge(s.rl_b, 1)
-    g.tensor.matmul(T.ps_o[:, 0:W], v_oth, T.sb[:, W:2 * W], False, True).then_inc(s.mm_o, 1)
+    g.tensor.wait_ge(s.arr_v, n_kv)
+    g.tensor.matmul(T.ps_o[:, 0:WC], v_oth, T.sb[:, WC:2 * WC], False, True).then_inc(s.mm_o, 1)
+    g.tensor.wait_ge(s.ldq, 16)
+    g.tensor.matmul(T.ps_c[:, 0:QP], k_own, T.qo[:], True, True).then_inc(s.mm_c, 1)
+    g.tensor.matmul(T.ps_c[:, QP:2 * QP], k_oth, T.qo[:], True, True).then_inc(s.mm_c, 1)
+    g.tensor.wait_ge(s.rl_c, 1)
+    g.tensor.matmul(T.ps_p[:, 0:QP], v_own, T.sbo[:, 0:QP], True, False)
+    g.tensor.matmul(T.ps_p[:, 0:QP], v_oth, T.sbo[:, QP:2 * QP], False, True).then_inc(s.mm_p, 1)
 
     g.vector.wait_ge(s.zs, 1)
     g.vector.wait_ge(s.mm_a, 1)
-    g.vector.tensor_tensor(T.sb[:, 0:W], T.ps_a[:, 0:W], T.zero[:], AluOpType.max).then_inc(s.rl_a, 1)
+    g.vector.tensor_tensor(T.sb[:, 0:WC], T.ps_a[:, 0:WC], T.zero[:], relu).then_inc(s.rl_a, 1)
     g.vector.wait_ge(s.mm_b, 1)
-    g.vector.tensor_tensor(T.sb[:, W:2 * W], T.ps_b[:, 0:W], T.zero[:], AluOpType.max).then_inc(s.rl_b, 1)
+    g.vector.tensor_tensor(T.sb[:, WC:2 * WC], T.ps_b[:, 0:WC], T.zero[:], relu).then_inc(s.rl_b, 1)
     g.vector.wait_ge(s.mm_o, 1)
-    g.vector.tensor_copy(T.yb[:], T.ps_o[:, 0:W]).then_inc(s.cp, 1)
+    g.vector.tensor_copy(T.yb[:], T.ps_o[:, 0:WC]).then_inc(s.cp, 1)
+    g.vector.wait_ge(s.mm_c, 2)
+    g.vector.tensor_tensor(T.sbo[:], T.ps_c[:, 0:2 * QP], T.zero[:, 0:2 * QP], relu).then_inc(s.rl_c, 1)
+    g.vector.wait_ge(s.mm_p, 1)
+    g.vector.tensor_copy(T.ybo[:], T.ps_p[:, 0:QP]).then_inc(s.cpo, 1)
 
     masks = _y_masks(T, topo, rank, clients)
     transfers = []
     for i, c in enumerate(clients):
         rid, pid = topo.addr(cores[c], core)
         transfers.append(RemoteDMATransfer(dst_ids=[DstId(rid=rid, pnc=pid)], dma_engine_mask=masks[i],
-                                           remote_sem=s.arr_y, src=T.yb[:, (i + 1) * QP:(i + 2) * QP],
-                                           dst=T.yland[:]))
+                                           remote_sem=s.arr_y, src=T.yb[:, i * QP:(i + 1) * QP], dst=T.yland[:]))
         sent += len(_engines(masks[i]))
     g.wait_ge(s.cp, 1)
     g.remote_dma_fused(transfers, local_sem=s.sent)
-    g.sync.wait_ge(s.cp, 1)
-    g.sync.dma_start(T.y[:], T.yb[:, 0:QP]).then_inc(s.st, 16)
+
+    g.sync.wait_ge(s.cpo, 1)
+    g.sync.dma_start(T.y[:], T.ybo[:]).then_inc(s.st, 16)
 
     g.wait_ge(s.sent, sent)
     g.wait_ge(s.st, 16)
@@ -122,7 +148,7 @@ def _client(g, core, T, topo, rank, server, clients):
     rid, pid = topo.addr(cores[server], core)
     mk = topo.mask(core, cores[server])
     g.wait_ge(s.ldq, 16)
-    g.remote_dma(out_ap=T.qall[:, (slot + 1) * QP:(slot + 2) * QP], in_ap=T.qd[:], remote_sem=s.arr_q,
+    g.remote_dma(out_ap=T.qc[:, slot * QP:(slot + 1) * QP], in_ap=T.qd[:], remote_sem=s.arr_q,
                  local_sem=s.sent, pid=pid, routing_id=rid, dma_engine_mask=mk)
     n_y = len(_engines(_y_masks(T, topo, server, clients)[slot]))
     g.sync.wait_ge(s.arr_y, n_y)

from concourse.bass import DstId, RemoteDMATransfer
from concourse.mybir import AluOpType

QP = 32
KP = 128
CAP = 2
WC = QP * CAP

SCRATCH = {
    "kd": ("dram", [128, KP], "bfloat16"),
    "vd": ("dram", [128, KP], "bfloat16"),
    "kv": ("sbuf", [128, 2 * KP], "bfloat16"),
    "kvo": ("sbuf", [128, 2 * KP], "bfloat16"),
    "qc": ("sbuf", [128, WC], "bfloat16"),
    "qo": ("sbuf", [128, QP], "bfloat16"),
    "qd": ("dram", [128, QP], "bfloat16"),
    "zero": ("sbuf", [128, WC], "float32"),
    "sb": ("sbuf", [128, 2 * WC], "bfloat16"),
    "sbo": ("sbuf", [128, 2 * QP], "bfloat16"),
    "yb": ("sbuf", [128, WC], "bfloat16"),
    "ybo": ("sbuf", [128, QP], "bfloat16"),
    "yland": ("dram", [128, QP], "bfloat16"),
    "ps_a": ("psum", [128, 512], "float32"),
    "ps_b": ("psum", [128, 512], "float32"),
    "ps_o": ("psum", [128, 512], "float32"),
    "ps_c": ("psum", [128, 512], "float32"),
    "ps_p": ("psum", [128, 512], "float32"),
}
SEMAPHORES = ["stk", "stv", "ldk", "ldv", "ldq", "zs", "arr_k", "arr_v", "arr_q", "arr_y",
              "mm_a", "mm_b", "rl_a", "rl_b", "mm_o", "cp", "mm_c", "rl_c", "mm_p", "cpo", "sent", "st"]


def _engines(mask):
    return [e for e in range(mask.bit_length()) if (mask >> e) & 1]


def _split(mask, parts):
    eng = _engines(mask)
    per = 1
    while per * 2 * parts <= len(eng):
        per *= 2
    return [sum(1 << e for e in eng[i * per:(i + 1) * per]) for i in range(parts)]


def _plan(T, topo):
    cores, mem = T.cores, list(T.tables["MEM"])
    served = {m: [] for m in mem}
    left = []
    for r in range(len(cores)):
        if r in mem:
            continue
        near = [m for m in mem if topo.same_plane(cores[r], cores[m]) and len(served[m]) < CAP]
        if near:
            served[near[0]].append(r)
        else:
            left.append(r)
    for r in left:
        served[min(mem, key=lambda m: len(served[m]))].append(r)
    return mem, served


def _y_masks(T, topo, server, clients):
    common = topo.mask(T.cores[server], T.cores[clients[0]])
    for c in clients:
        common &= topo.mask(T.cores[server], T.cores[c])
    return _split(common, len(clients))


def _memory_rank(g, core, T, topo, rank, mem, served):
    s, cores = T.sem, T.cores
    other = [m for m in mem if m != rank][0]
    clients = served[rank]
    k_own, v_own = T.kv[:, 0:KP], T.kv[:, KP:2 * KP]
    k_oth, v_oth = T.kvo[:, 0:KP], T.kvo[:, KP:2 * KP]
    relu = AluOpType.max

    g.sync.dma_start(T.kd[:], T.k[:]).then_inc(s.stk, 16)
    g.scalar.dma_start(T.vd[:], T.v[:]).then_inc(s.stv, 16)
    g.sync.dma_start(k_own, T.k[:]).then_inc(s.ldk, 16)
    g.scalar.dma_start(v_own, T.v[:]).then_inc(s.ldv, 16)
    g.sync.dma_start(T.qo[:], T.q[:]).then_inc(s.ldq, 16)
    g.vector.memset(T.zero[:], 0.0).then_inc(s.zs, 1)

    rid, pid = topo.addr(cores[other], core)
    mk = topo.mask(core, cores[other])
    g.wait_ge(s.stk, 16)
    g.remote_dma(out_ap=k_oth, in_ap=T.kd[:], remote_sem=s.arr_k, local_sem=s.sent,
                 pid=pid, routing_id=rid, dma_engine_mask=mk)
    g.wait_ge(s.stv, 16)
    g.remote_dma(out_ap=v_oth, in_ap=T.vd[:], remote_sem=s.arr_v, local_sem=s.sent,
                 pid=pid, routing_id=rid, dma_engine_mask=mk)
    sent = 2 * len(_engines(mk))

    n_q = sum(len(_engines(topo.mask(cores[c], core))) for c in clients)
    n_kv = len(_engines(topo.mask(cores[other], core)))

    g.tensor.wait_ge(s.ldk, 16)
    g.tensor.wait_ge(s.arr_q, n_q)
    g.tensor.matmul(T.ps_a[:, 0:WC], k_own, T.qc[:], True, True).then_inc(s.mm_a, 1)
    g.tensor.wait_ge(s.arr_k, n_kv)
    g.tensor.matmul(T.ps_b[:, 0:WC], k_oth, T.qc[:], True, True).then_inc(s.mm_b, 1)
    g.tensor.wait_ge(s.ldv, 16)
    g.tensor.wait_ge(s.rl_a, 1)
    g.tensor.matmul(T.ps_o[:, 0:WC], v_own, T.sb[:, 0:WC], True, False)
    g.tensor.wait_ge(s.rl_b, 1)
    g.tensor.wait_ge(s.arr_v, n_kv)
    g.tensor.matmul(T.ps_o[:, 0:WC], v_oth, T.sb[:, WC:2 * WC], False, True).then_inc(s.mm_o, 1)
    g.tensor.wait_ge(s.ldq, 16)
    g.tensor.matmul(T.ps_c[:, 0:QP], k_own, T.qo[:], True, True).then_inc(s.mm_c, 1)
    g.tensor.matmul(T.ps_c[:, QP:2 * QP], k_oth, T.qo[:], True, True).then_inc(s.mm_c, 1)
    g.tensor.wait_ge(s.rl_c, 1)
    g.tensor.matmul(T.ps_p[:, 0:QP], v_own, T.sbo[:, 0:QP], True, False)
    g.tensor.matmul(T.ps_p[:, 0:QP], v_oth, T.sbo[:, QP:2 * QP], False, True).then_inc(s.mm_p, 1)

    g.vector.wait_ge(s.zs, 1)
    g.vector.wait_ge(s.mm_a, 1)
    g.vector.tensor_tensor(T.sb[:, 0:WC], T.ps_a[:, 0:WC], T.zero[:], relu).then_inc(s.rl_a, 1)
    g.vector.wait_ge(s.mm_b, 1)
    g.vector.tensor_tensor(T.sb[:, WC:2 * WC], T.ps_b[:, 0:WC], T.zero[:], relu).then_inc(s.rl_b, 1)
    g.vector.wait_ge(s.mm_o, 1)
    g.vector.tensor_copy(T.yb[:], T.ps_o[:, 0:WC]).then_inc(s.cp, 1)
    g.vector.wait_ge(s.mm_c, 2)
    g.vector.tensor_tensor(T.sbo[:], T.ps_c[:, 0:2 * QP], T.zero[:, 0:2 * QP], relu).then_inc(s.rl_c, 1)
    g.vector.wait_ge(s.mm_p, 1)
    g.vector.tensor_copy(T.ybo[:], T.ps_p[:, 0:QP]).then_inc(s.cpo, 1)

    masks = _y_masks(T, topo, rank, clients)
    transfers = []
    for i, c in enumerate(clients):
        rid, pid = topo.addr(cores[c], core)
        transfers.append(RemoteDMATransfer(dst_ids=[DstId(rid=rid, pnc=pid)], dma_engine_mask=masks[i],
                                           remote_sem=s.arr_y, src=T.yb[:, i * QP:(i + 1) * QP], dst=T.yland[:]))
        sent += len(_engines(masks[i]))
    g.wait_ge(s.cp, 1)
    g.remote_dma_fused(transfers, local_sem=s.sent)

    g.sync.wait_ge(s.cpo, 1)
    g.sync.dma_start(T.y[:], T.ybo[:]).then_inc(s.st, 16)

    g.wait_ge(s.sent, sent)
    g.wait_ge(s.st, 16)


def _client(g, core, T, topo, rank, server, clients):
    s, cores = T.sem, T.cores
    slot = clients.index(rank)
    g.sync.dma_start(T.qd[:], T.q[:]).then_inc(s.ldq, 16)
    rid, pid = topo.addr(cores[server], core)
    mk = topo.mask(core, cores[server])
    g.wait_ge(s.ldq, 16)
    g.remote_dma(out_ap=T.qc[:, slot * QP:(slot + 1) * QP], in_ap=T.qd[:], remote_sem=s.arr_q,
                 local_sem=s.sent, pid=pid, routing_id=rid, dma_engine_mask=mk)
    n_y = len(_engines(_y_masks(T, topo, server, clients)[slot]))
    g.sync.wait_ge(s.arr_y, n_y)
    g.sync.dma_start(T.y[:], T.yland[:]).then_inc(s.st, 16)
    g.wait_ge(s.sent, len(_engines(mk)))
    g.wait_ge(s.st, 16)


def rank_program(g, core, T, topo):
    rank = T.rank_of(core)
    if rank is None:
        return
    mem, served = _plan(T, topo)
    if rank in mem:
        _memory_rank(g, core, T, topo, rank, mem, served)
    else:
        server = [m for m in mem if rank in served[m]][0]
        _client(g, core, T, topo, rank, server, served[server])
